import numpy as np
import ml_dtypes


def mxq(x, axis, fmt="e4m3"):
    dtype, down = {"e4m3": (ml_dtypes.float8_e4m3fn, 7), "e5m2": (ml_dtypes.float8_e5m2, 14)}[fmt]
    v = np.moveaxis(np.asarray(x, np.float32).astype(ml_dtypes.bfloat16).astype(np.float64), axis, -1)
    blocks = v.reshape(v.shape[:-1] + (-1, 32))
    amax = np.abs(blocks).max(-1, keepdims=True)
    byte = np.maximum(np.where(amax > 0, np.frexp(amax)[1] - 1 + 127, 0) - down, 1)
    scale = np.exp2(byte - 127.0)
    codes = (blocks / scale).astype(np.float32).astype(dtype).astype(np.float64)
    return np.moveaxis((codes * scale).reshape(v.shape), -1, axis)


WIDE = False


def mx_kscale(k):
    if not WIDE:
        return np.ones(k)
    levels = np.array([10, -10, 5, -5, 0])
    if k % 512:
        return np.exp2(np.random.permutation(np.resize(levels, k // 32))).repeat(32)
    a = np.empty((k // 512, 16))
    for p in range(k // 512):
        a[p, :8] = np.random.permutation(np.resize(levels, 8))
        for g in range(8):
            far = levels[np.abs(levels - a[p, g]) >= 10]
            a[p, g + 8] = far[np.random.randint(len(far))]
    return np.exp2(a.ravel()).repeat(32)


def f64(x):
    return np.asarray(x).astype(np.float64)


def striped(idx):
    return np.tile(np.asarray(idx).reshape(-1, 16).T, (8, 1)).astype(np.uint16)


def unstriped(offs):
    return offs[:16].T.reshape(-1).astype(np.int64)


E2M1 = np.array([0.0, 0.5, 1.0, 1.5, 2.0, 3.0, 4.0, 6.0, -0.0, -0.5, -1.0, -1.5, -2.0, -3.0, -4.0, -6.0])


def pack_weight(w, fmt):
    k, n = w.shape
    w = f64(np.asarray(w, np.float32).astype(ml_dtypes.bfloat16)).reshape(k // 32, 32, n)
    amax = np.abs(w).max(1)
    if fmt == "e4m3":
        byte = np.frexp(amax)[1] - 1 + 127 - 7
    else:
        mant, ex = np.frexp(amax / 6.0)
        byte = np.where(mant > 0.5, ex, ex - 1) + 127
    byte = np.clip(np.where(amax > 0, byte, 1), 1, 254)
    scaled = (w * np.exp2(127.0 - byte)[:, None, :]).reshape(k, n).astype(np.float32)
    by_word = np.ascontiguousarray(scaled.reshape(k // 512, 128, 4, n).transpose(0, 1, 3, 2))
    if fmt == "e4m3":
        words = by_word.astype(ml_dtypes.float8_e4m3fn).view(np.uint8)
    else:
        c = by_word.astype(ml_dtypes.float4_e2m1fn).view(np.uint8) & 0xF
        words = (c[..., 0::2] | (c[..., 1::2] << 4)).reshape(k // 512, 128, 2 * n)
    return np.ascontiguousarray(words), np.ascontiguousarray(byte.astype(np.uint8).reshape(k // 512, 16, n))


def unpack_weight(words, scales, fmt):
    g, _, n = scales.shape
    words = np.ascontiguousarray(words).reshape(g, 128, n, -1)
    if fmt == "e4m3":
        vals = words.view(ml_dtypes.float8_e4m3fn).astype(np.float64)
    else:
        nib = np.empty((g, 128, n, 4), np.uint8)
        nib[..., 0::2] = words & 0xF
        nib[..., 1::2] = words >> 4
        vals = E2M1[nib]
    vals = vals * np.repeat(np.exp2(scales.astype(np.float64) - 127.0), 8, axis=1)[..., None]
    return vals.transpose(0, 1, 3, 2).reshape(g * 512, n)


B, N, T, D, DV, NQ = 1, 512, 1024, 512, 0, 128
PAGE = 16
SEG = 16


def setup_inputs():
    n = np.random.standard_normal
    pages = np.random.permutation(T // PAGE)[:B * N // PAGE]
    idx = (pages[:, None] * PAGE + np.arange(PAGE)[None, :]).reshape(-1)
    s = mx_kscale(D)[:, None]
    kp = pack_weight(n((D, T)) / s, "e4m3")
    return {
        "qT": (n((B, D, NQ)) * s * (1.00 / np.sqrt(D))).astype(np.float32),
        "k_words": kp[0],
        "k_scales": kp[1],
        "kb": np.tile(n(T), (128, 1)).astype(np.float32),
        "offs": striped(idx),
    }


def reference(qT, k_words, k_scales, kb, offs):
    idx = unstriped(offs)
    pool = unpack_weight(k_words, k_scales, "e4m3")
    pick = lambda x: x[:, idx].reshape(x.shape[0], B, N).transpose(1, 0, 2)
    a = mxq(f64(qT), 1, "e4m3").transpose(0, 2, 1) @ pick(pool)
    a = a + pick(f64(kb))[:, :1, :]
    return a.reshape(B, NQ, N // SEG, SEG).max(-1)

@@ -1,0 +1,105 @@
+from contextlib import ExitStack
+
+import concourse.mybir as mybir
+
+P = 128
+PACK = 4
+T = 1024
+N = 512
+NQ = 128
+D = 512
+SEG = 16
+HALF = N // 2
+LIST_COLS = N // 16
+
+FLOPS = 2 * D * NQ * N
+
+F32 = mybir.dt.float32
+BF16 = mybir.dt.bfloat16
+I32 = mybir.dt.int32
+U32 = mybir.dt.uint32
+U16 = mybir.dt.uint16
+U8 = mybir.dt.uint8
+FP8X4 = mybir.dt.float8_e4m3fn_x4
+ADD = mybir.AluOpType.add
+MAX = mybir.AluOpType.max
+
+
+def tile_attend_maxsim_kb_kernel(tc, qT, k_words, k_scales, kb, offs, out):
+    nc = tc.nc
+    with ExitStack() as ctx:
+        held = ctx.enter_context(tc.tile_pool(name="held", bufs=1))
+        psum = ctx.enter_context(tc.psum_pool(name="psum", bufs=1))
+
+        offsets = held.tile([P, LIST_COLS], U16, name="offsets")
+        nc.sync.dma_start(offsets[:], offs)
+
+        pool_scales = held.tile([P, T // 4], I32, name="pool_scales", align_bytes=64)
+        nc.vector.memset(pool_scales[:], 0)
+        for quad in range(4):
+            nc.scalar.dma_start(
+                pool_scales[32 * quad : 32 * quad + 4, :],
+                k_scales[0, 4 * quad : 4 * quad + 4, :].bitcast(I32),
+            )
+
+        q_raw = held.tile([P, PACK, NQ], F32, name="q_raw", align_bytes=64)
+        nc.sync.dma_start(q_raw[:], qT[0].rearrange("(p j) w -> p j w", j=PACK))
+
+        pool_words = held.tile([P, T], I32, name="pool_words", align_bytes=64)
+        nc.sync.dma_start(pool_words[:], k_words[0].rearrange("p t r -> p (t r)").bitcast(I32))
+
+        pool_bias = held.tile([P, T], F32, name="pool_bias", align_bytes=64)
+        nc.sync.dma_start(pool_bias[:], kb)
+
+        q_grouped = held.tile([P, NQ, PACK], BF16, name="q_grouped", align_bytes=64)
+        nc.scalar.copy(q_grouped[:], q_raw[:].rearrange("p j w -> p w j"))
+
+        key_scales = held.tile([P, N], U8, name="key_scales", align_bytes=64)
+        nc.vector.tensor_copy(key_scales[:], pool_scales[:].bitcast(U8).indirect(offsets[:]))
+
+        q_codes = held.tile([P, NQ], U32, name="q_codes", align_bytes=64)
+        q_scales = held.tile([P, NQ], U8, name="q_scales", align_bytes=64)
+        nc.vector.quantize_mx(
+            out=q_codes[:].bitcast(FP8X4),
+            scales=q_scales[:],
+            in_=q_grouped[:].rearrange("p w j -> p (w j)"),
+        )
+
+        lists = [offsets[:, h * LIST_COLS // 2 : (h + 1) * LIST_COLS // 2] for h in range(2)]
+        banks = []
+        for h in range(2):
+            key_words = held.tile([P, HALF], U32, name=f"key_words{h}", align_bytes=64)
+            nc.vector.tensor_copy(key_words[:], pool_words[:].bitcast(U32).indirect(lists[h]))
+            bank = psum.tile([P, HALF], F32, name=f"bank{h}")
+            nc.tensor.matmul_mx(
+                out=bank[:],
+                lhsT=q_codes[:].bitcast(FP8X4),
+                lhsT_scale=q_scales[:],
+                rhs=key_words[:].bitcast(FP8X4),
+                rhs_scale=key_scales[:, h * HALF : (h + 1) * HALF],
+                start=True,
+                stop=True,
+            )
+            banks.append(bank)
+
+        biases = []
+        for h in range(2):
+            bias = held.tile([P, HALF], F32, name=f"bias{h}", align_bytes=64)
+            nc.vector.tensor_copy(bias[:], pool_bias[:].indirect(lists[h]))
+            biases.append(bias)
+
+        scores = []
+        for h in range(2):
+            score = held.tile([P, HALF], F32, name=f"score{h}", align_bytes=64)
+            nc.vector.tensor_tensor(score[:], banks[h][:], biases[h][:], ADD)
+            scores.append(score)
+
+        best = held.tile([P, N // SEG], F32, name="best", align_bytes=64)
+        for h in range(2):
+            nc.vector.tensor_reduce(
+                best[:, h * HALF // SEG : (h + 1) * HALF // SEG],
+                scores[h][:].rearrange("p (j s) -> p j s", s=SEG),
+                mybir.AxisListType.X,
+                MAX,
+            )
+        nc.sync.dma_start(out[0], best[:])

@@ -36,14 +36,16 @@ def tile_attend_maxsim_kb_kernel(tc, qT, k_words, k_scales, kb, offs, out):
 
         pool_scales = held.tile([P, T // 4], I32, name="pool_scales", align_bytes=64)
         nc.vector.memset(pool_scales[:], 0)
-        for quad in range(4):
-            nc.scalar.dma_start(
-                pool_scales[32 * quad : 32 * quad + 4, :],
-                k_scales[0, 4 * quad : 4 * quad + 4, :].bitcast(I32),
-            )
 
         q_raw = held.tile([P, PACK, NQ], F32, name="q_raw", align_bytes=64)
         nc.sync.dma_start(q_raw[:], qT[0].rearrange("(p j) w -> p j w", j=PACK))
+
+        for quad in range(4):
+            queue = nc.sync if quad < 2 else nc.scalar
+            queue.dma_start(
+                pool_scales[32 * quad : 32 * quad + 4, :],
+                k_scales[0, 4 * quad : 4 * quad + 4, :].bitcast(I32),
+            )
 
         pool_words = held.tile([P, T], I32, name="pool_words", align_bytes=64)
         nc.sync.dma_start(pool_words[:], k_words[0].rearrange("p t r -> p (t r)").bitcast(I32))

from contextlib import ExitStack

import concourse.mybir as mybir

P = 128
PACK = 4
T = 1024
N = 512
NQ = 128
D = 512
SEG = 16
HALF = N // 2
LIST_COLS = N // 16

FLOPS = 2 * D * NQ * N

F32 = mybir.dt.float32
BF16 = mybir.dt.bfloat16
I32 = mybir.dt.int32
U32 = mybir.dt.uint32
U16 = mybir.dt.uint16
U8 = mybir.dt.uint8
FP8X4 = mybir.dt.float8_e4m3fn_x4
ADD = mybir.AluOpType.add
MAX = mybir.AluOpType.max


def tile_attend_maxsim_kb_kernel(tc, qT, k_words, k_scales, kb, offs, out):
    nc = tc.nc
    with ExitStack() as ctx:
        held = ctx.enter_context(tc.tile_pool(name="held", bufs=1))
        psum = ctx.enter_context(tc.psum_pool(name="psum", bufs=1))

        offsets = held.tile([P, LIST_COLS], U16, name="offsets")
        nc.sync.dma_start(offsets[:], offs)

        pool_scales = held.tile([P, T // 4], I32, name="pool_scales", align_bytes=64)
        nc.vector.memset(pool_scales[:], 0)

        q_raw = held.tile([P, PACK, NQ], F32, name="q_raw", align_bytes=64)
        nc.sync.dma_start(q_raw[:], qT[0].rearrange("(p j) w -> p j w", j=PACK))

        for quad in range(4):
            queue = nc.sync if quad < 2 else nc.scalar
            queue.dma_start(
                pool_scales[32 * quad : 32 * quad + 4, :],
                k_scales[0, 4 * quad : 4 * quad + 4, :].bitcast(I32),
            )

        pool_words = held.tile([P, T], I32, name="pool_words", align_bytes=64)
        nc.sync.dma_start(pool_words[:], k_words[0].rearrange("p t r -> p (t r)").bitcast(I32))

        pool_bias = held.tile([P, T], F32, name="pool_bias", align_bytes=64)
        nc.sync.dma_start(pool_bias[:], kb)

        q_grouped = held.tile([P, NQ, PACK], BF16, name="q_grouped", align_bytes=64)
        nc.scalar.copy(q_grouped[:], q_raw[:].rearrange("p j w -> p w j"))

        key_scales = held.tile([P, N], U8, name="key_scales", align_bytes=64)
        nc.vector.tensor_copy(key_scales[:], pool_scales[:].bitcast(U8).indirect(offsets[:]))

        q_codes = held.tile([P, NQ], U32, name="q_codes", align_bytes=64)
        q_scales = held.tile([P, NQ], U8, name="q_scales", align_bytes=64)
        nc.vector.quantize_mx(
            out=q_codes[:].bitcast(FP8X4),
            scales=q_scales[:],
            in_=q_grouped[:].rearrange("p w j -> p (w j)"),
        )

        lists = [offsets[:, h * LIST_COLS // 2 : (h + 1) * LIST_COLS // 2] for h in range(2)]
        banks = []
        for h in range(2):
            key_words = held.tile([P, HALF], U32, name=f"key_words{h}", align_bytes=64)
            nc.vector.tensor_copy(key_words[:], pool_words[:].bitcast(U32).indirect(lists[h]))
            bank = psum.tile([P, HALF], F32, name=f"bank{h}")
            nc.tensor.matmul_mx(
                out=bank[:],
                lhsT=q_codes[:].bitcast(FP8X4),
                lhsT_scale=q_scales[:],
                rhs=key_words[:].bitcast(FP8X4),
                rhs_scale=key_scales[:, h * HALF : (h + 1) * HALF],
                start=True,
                stop=True,
            )
            banks.append(bank)

        biases = []
        for h in range(2):
            bias = held.tile([P, HALF], F32, name=f"bias{h}", align_bytes=64)
            nc.vector.tensor_copy(bias[:], pool_bias[:].indirect(lists[h]))
            biases.append(bias)

        scores = []
        for h in range(2):
            score = held.tile([P, HALF], F32, name=f"score{h}", align_bytes=64)
            nc.vector.tensor_tensor(score[:], banks[h][:], biases[h][:], ADD)
            scores.append(score)

        best = held.tile([P, N // SEG], F32, name="best", align_bytes=64)
        for h in range(2):
            nc.vector.tensor_reduce(
                best[:, h * HALF // SEG : (h + 1) * HALF // SEG],
                scores[h][:].rearrange("p (j s) -> p j s", s=SEG),
                mybir.AxisListType.X,
                MAX,
            )
        nc.sync.dma_start(out[0], best[:])
